import numpy as np, ml_dtypes
CORES = [3,11,19,27,35,43,51,59]
N = 8
BF = ml_dtypes.bfloat16
W, C, B, VI, S = 4096, 4096, 192, 4, 3
def parts(rng):
    rt = rng.integers(0, 16, (N, 8, 16, W)); pf = rng.integers(0, W, (N, 8, 16, C))
    jc = np.argsort(rng.random((N, 8, C)), axis=-1)[..., :16 * B].reshape(N, 8, 16, B)
    return rt, pf, jc, rng.integers(0, 16, (N, 8, 16, B)), rng.integers(0, 16, (N, 8, B))
def pack(rt, pf, jc, fx, sr):
    return {"rt": np.ascontiguousarray(rt.reshape(N, 128, W)).astype(np.float32).astype(BF),
            "pk": np.ascontiguousarray((pf[..., :C // 2] + 4096 * pf[..., C // 2:]).reshape(N, 128, C // 2)).astype(np.int32),
            "jc": np.ascontiguousarray(jc.reshape(N, 128, B)).astype(np.int32),
            "fx": np.ascontiguousarray(fx.reshape(N, 128, B)).astype(np.float32).astype(BF), "sr": np.ascontiguousarray(sr).astype(np.int32)}
def setup_inputs(rng):
    return pack(*parts(rng))
def setup_inputs_ties(rng):
    rt, pf, jc, fx, sr = parts(rng)
    pool = rng.integers(0, 16, (N, 8, 16, 8)); pool[:, 1::2] = rng.integers(0, 2, (N, 4, 16, 8))
    rt = np.take_along_axis(pool, rng.integers(0, 8, (N, 8, 1, W)), 3)
    fx = np.where(rng.random((N, 8, 1, B)) < 0.5, np.take_along_axis(pool, rng.integers(0, 8, (N, 8, 1, B)), 3), fx)
    q = rng.permutation(C)[:C // 8]; pf[..., q] = pf[:, :, :1, q]
    return pack(rt, pf, jc, fx, sr)
def setup_inputs_rounds(rng):
    rt, pf, jc, fx, sr = parts(rng); h = W // 2
    o = np.argsort(rng.random((N, 8, W)), axis=-1); light = np.zeros((N, 8, W), bool); np.put_along_axis(light, o[..., :h], True, 2)
    rt = np.where(light[:, :, None, :], rng.integers(0, 2, (N, 8, 16, W)), rng.integers(8, 16, (N, 8, 16, W)))
    ln = rng.integers(1, S + 2, (8, B)); back = (rng.random((8, B)) * ln).astype(np.int64)
    ln[0] = S; back[0] = 0; ln[1] = S + 1; ln[2] = 1; back[2] = 0
    if np.count_nonzero(ln <= S) % 2 == 0:
        ln[3, 0] = S + 1 if ln[3, 0] <= S else S; back[3, 0] = 0
    s0 = rng.integers(0, 16, (8, B)); a = (np.arange(16)[None, :, None] - s0[:, None, :]) % 16
    nxt = (np.where(a == ln[:, None, :] - 1, back[:, None, :], a + 1) + s0[:, None, :]) % 16
    pc = np.argsort(rng.random((8, C)), axis=-1)[:, :16 * B]
    kap = rng.integers(0, 16, (8, C)); np.put_along_axis(kap, pc, nxt.reshape(8, 16 * B), 1)
    one = kap[None, :, None, :] == np.arange(16)[None, None, :, None]
    pf = np.take_along_axis(o[:, :, None, :], rng.integers(0, h, (N, 8, 16, C)) + np.where(one, 0, h), 3)
    e = np.argsort(rng.random((N, 8, B)), axis=-1)
    jc = np.take_along_axis(np.broadcast_to(pc.reshape(1, 8, 16, B), (N, 8, 16, B)), np.broadcast_to(e[:, :, None, :], (N, 8, 16, B)), 3)
    sr = np.take_along_axis(np.broadcast_to(s0[None], (N, 8, B)), e, 2)
    return pack(rt, pf, jc, rng.integers(0, 2, (N, 8, 16, B)), sr)
def setup_inputs_full(rng):
    h = W // 2; u = h // 2; rows = np.arange(16)
    side = (np.arange(N)[:, None] + np.arange(8)[None, :]) % 2 * h
    o = np.argsort(rng.random((N, 8, h)), axis=-1) + side[:, :, None]; light = np.zeros((N, 8, W), bool); np.put_along_axis(light, o[..., :u], True, 2)
    rt = np.where(light[:, :, None, :], rng.integers(0, 2, (N, 8, 16, W)), rng.integers(8, 16, (N, 8, 16, W)))
    s0 = 2 * rng.permutation(8) + rng.integers(0, 2, 8); a = (rows[None, :] - s0[:, None]) % 16
    nxt = (np.where(a == S - 1, 0, a + 1) + s0[:, None]) % 16
    lower = np.argsort(rng.random((8, C // 2)), axis=-1)[:, :8 * B]; upper = np.argsort(rng.random((8, C // 2)), axis=-1)[:, :8 * B] + C // 2
    pc = np.concatenate([lower, upper], axis=1).reshape(8, 16, B)
    kap = rng.integers(0, 16, (N, 8, C))
    np.put_along_axis(kap, np.broadcast_to(pc.reshape(1, 8, 16 * B), (N, 8, 16 * B)), np.broadcast_to(np.repeat(nxt, B, axis=1)[None], (N, 8, 16 * B)), 2)
    whole = int(rng.integers(0, 8))
    for g in range(8):
        if g != whole: kap[1::2, g, int(pc[g, (s0[g] + S - 1) % 16, 0])] = (s0[g] + S) % 16
    one = kap[:, :, None, :] == rows[None, None, :, None]
    pf = np.take_along_axis(o[:, :, None, :], rng.integers(0, u, (N, 8, 16, C)) + np.where(one, 0, u), 3)
    e = np.argsort(rng.random((N, 8, 16, B)), axis=-1)
    jc = np.take_along_axis(np.broadcast_to(pc[None], (N, 8, 16, B)), e, 3)
    return pack(rt, pf, jc, rng.integers(0, 2, (N, 8, 16, B)), np.broadcast_to(s0[None, :, None], (N, 8, B)))
def setup_inputs_ends(rng):
    rt, pf, jc, fx, sr = parts(rng)
    pf[:, ::2] = rng.choice(np.array([0, 1, W // 2, W - 1]), (N, 4, 16, C)); pf[:, 1::2, :, C // 2 - 1] = W - 1; pf[:, 1::2, :, C - 1] = W - 1
    jc[:, ::2] = np.concatenate([np.arange(8 * B), np.arange(C - 8 * B, C)]).reshape(16, B)
    rt[:, 1::2] = 15 * rng.integers(0, 2, (N, 4, 16, W)); fx = 15 * rng.integers(0, 2, (N, 8, 16, B)); sr = 15 * rng.integers(0, 2, (N, 8, B))
    o = rng.permutation(W); n = B // 2; hi = o[:W // 4]; mid = o[W // 4:W // 2]; lo = o[W // 2:3 * W // 4]
    rt[:, 1][:, :, hi] = 15; rt[:, 1][:, :, mid] = 14; rt[:, 1][:, :, lo] = 0
    for q in range(N):
        x = rng.permutation(B)[:n]; p = np.argsort(rng.random((16, n)), axis=0)[:3]; c = jc[q, 1, p, x]
        for i, k, a, b in ((0, p[1], mid, hi), (1, p[2], hi, lo), (2, p[1], lo, hi)):
            pf[q, 1][:, c[i]] = rng.choice(b, (16, n)); pf[q, 1][k, c[i]] = rng.choice(a, n)
        fx[q, 1][:, x] = 0; sr[q, 1][x] = p[0]
    return pack(rt, pf, jc, fx, sr)
def setup_inputs_spread(rng):
    rt, pf, jc, fx, sr = parts(rng)
    rt = np.minimum((16 * rng.random((N, 8, 16, W)) ** np.exp2(rng.integers(-2, 4, (N, 8, 1, W)))).astype(np.int64), 15)
    pf = np.minimum((W * rng.random((N, 8, 16, C)) ** np.exp2(rng.integers(-2, 4, (N, 8, 1, C)))).astype(np.int64), W - 1)
    fx = np.minimum((16 * rng.random((N, 8, 16, B)) ** np.exp2(rng.integers(-2, 4, (N, 8, 1, B)))).astype(np.int64), 15)
    sr = np.minimum((16 * rng.random((N, 8, B)) ** np.exp2(rng.integers(-1, 3, (N, 8, 1)))).astype(np.int64), 15)
    return pack(rt, pf, jc, fx, sr)
def check_inputs(d):
    bad = []
    for k in ("rt", "fx"):
        a = np.asarray(d[k]).astype(np.float32)
        if not np.all((a >= 0) & (a <= 15) & (a == np.floor(a))): bad.append("whole numbers of " + k)
    a = np.asarray(d["pk"]).astype(np.int64)
    if np.min(a) < 0 or np.max(a & 4095) >= W or np.max(a >> 12) >= W: bad.append("range of pk")
    for k, hi in (("jc", C - 1), ("sr", 15)):
        if np.min(d[k]) < 0 or np.max(d[k]) > hi: bad.append("range of " + k)
    s = np.sort(np.asarray(d["jc"]).reshape(N, 8, 16 * B), axis=-1)
    if np.any(s[..., 1:] == s[..., :-1]): bad.append("courts of a group differ")
    return bad
def reference(rt, pk, jc, fx, sr):
    R = rt.astype(np.float32).astype(np.int32).reshape(N, 8, 16, W); f = fx.astype(np.float32).astype(np.int32).reshape(N, 8, 16, B)
    two = pk.astype(np.int32).reshape(N, 8, 16, C // 2); pf = np.concatenate([two & 4095, two >> 12], axis=3)
    J = jc.astype(np.int32).reshape(N, 8, 16, B); start = sr.astype(np.int32); Z = np.zeros(N, np.int32); rows = np.arange(16, dtype=np.int32)
    for t in range(VI):
        if t > 0:
            f = np.roll(f, 1, axis=0); J = np.roll(J, 1, axis=0); start = np.roll(start, 1, axis=0)
        m = np.zeros((N, 8, 16, B), np.int32); v = np.zeros((N, 8, 16, B), np.int32); num = np.zeros((N, 8, 16, B), np.int32)
        p = start; go = np.ones((N, 8, B), bool); first = np.zeros((N, 8, B), np.int32); new = np.zeros((N, 8, B), np.int32)
        for s in range(1, S + 1):
            c = np.take_along_axis(J, p[:, :, None, :], 2)
            n = np.take_along_axis(pf, np.broadcast_to(c, (N, 8, 16, B)), 3)
            x = np.take_along_axis(R, np.broadcast_to(n.reshape(N, 8, 1, 16 * B), (N, 8, 16, 16 * B)), 3).reshape(N, 8, 16, 16, B)
            dist = np.add.reduce(np.abs(x - f[:, :, :, None, :]), axis=2)
            k = np.argmin(dist, axis=2).astype(np.int32)
            kk = k[:, :, None, :]; nk = np.take_along_axis(n, kk, 2)
            rule = np.take_along_axis(R, np.broadcast_to(nk, (N, 8, 16, B)), 3)
            here = (rows[None, None, :, None] == p[:, :, None, :]) & go[:, :, None, :]
            v = np.where(here, kk, v); num = np.where(here, nk, num); m = np.where(here, np.int32(s), m)
            f = np.where(go[:, :, None, :], np.abs(f - rule), f)
            mk = np.take_along_axis(m, kk, 2)[:, :, 0]; nr = np.take_along_axis(num, kk, 2)
            shut = go & (mk > 0)
            tot = np.add.reduce(np.take_along_axis(R, np.broadcast_to(nr, (N, 8, 16, B)), 3), axis=2)
            odd = ((tot + Z[:, None, None]) & 1) == 1
            new = np.where(shut, np.where(odd, nk[:, :, 0], nr[:, :, 0]), new); first = np.where(shut, mk, first)
            go = go & ~shut; p = np.where(go, k, p)
        closed = first > 0
        loop = closed[:, :, None, :] & (m >= first[:, :, None, :])
        at = np.broadcast_to(J.reshape(N, 8, 1, 16 * B), (N, 8, 16, 16 * B))
        old = np.take_along_axis(pf, at, 3).reshape(N, 8, 16, 16, B)
        hit = loop[:, :, None] & (v[:, :, None] == rows[None, None, :, None, None])
        np.put_along_axis(pf, at, np.where(hit, new[:, :, None, None, :], old).reshape(N, 8, 16, 16 * B), 3)
        Z = Z + np.add.reduce(closed.astype(np.int32), axis=(1, 2))
    return {"yp": (pf[..., :C // 2] + 4096 * pf[..., C // 2:]).reshape(N, 128, C // 2).astype(np.float32), "yf": f.reshape(N, 128, B).astype(np.float32).astype(BF)}

from concourse.mybir import dt, AluOpType, AxisListType, ActivationFunctionType

N = 8
VI = 4
NV = 8
KS = 3
F32, BF, I32T, U16 = "float32", "bfloat16", "int32", "uint16"
SIZES = {
    F32: "pkg0 204 pkg1 204 pkg2 204 pkg3 204 ones32 128 I32 128 BD32 128 W32 2048 pm 16 cols 8 M1 192 Me 192 Mo 192 KU 224 TA 192 "
         "TB 208 TC 208 t1 192 t2 192 t3 192 OH 192 Q0 192 Qs 192 rst 192 run 192 fw 1400 P24 24 P 80 Bv 576 yps 2048",
    BF: "rtb 4096 fin0 192 fin1 192 fin2 192 fin3 192 fo0 192 fo1 192 fo2 192 fo3 192 fa 192 fb 192 onesb 128 Ib 128 nI 128 zt 512 "
        "BDb 128 W65 2048 Vi 2048 DIAG 192 FX %d dall 9216 GC %d o3b 12 kb 12 kA 12 R 192 EQ 576" % (256 * NV, 256 * (12 - NV)),
    I32T: "pks 2048 pf 4480 jcs 192 pidx 4 CPi 192 i16 192 J256 12 D24 24 x12 12 r96 96 iw 640 kk2 12 kk3 12 K 80 sk 36 newv 384",
    U16: "exo 12 rk 6 rp 6 N16 192 c16_0 12 c16_1 12 c16n 12 L16 12 cl16 36",
}
SCRATCH = {
    "sr8": ("sbuf", [8, 192], I32T), "srb": ("sbuf", [8, 192], BF), "Sel": ("sbuf", [8, 128], BF), "D3": ("sbuf", [128, NV, 256], BF),
    "key": ("psum", [128, 512], F32), "psC": ("psum", [128, 4, 256], F32), "U": ("psum", [128, 1024], F32),
    "Wp": ("psum", [128, 512], F32), "mis": ("psum", [128, 512], F32),
}
for _ty in SIZES:
    _l = SIZES[_ty].split()
    for _i in range(0, len(_l), 2):
        SCRATCH[_l[_i]] = ("sbuf", [128, int(_l[_i + 1])], _ty)
SEMAPHORES = "cv cs ct cg ls pk1 pk2 pk3 fa1 fa2 fa3 dj ds df dp0 dp1 dr dyf dy0 dy1 dy2 dy3".split()


def rank_program(g, core, T, topo):
    rank = T.rank_of(core)
    if rank is None:
        return
    A, AF, X = AluOpType, ActivationFunctionType, AxisListType.X
    add, sub, mul, eq = A.add, A.subtract, A.mult, A.is_equal
    queues = {"v": g.vector, "s": g.scalar, "t": g.tensor, "g": g, "y": g.sync}
    csem = {"v": "cv", "s": "cs", "t": "ct", "g": "cg"}
    know = {q: {} for q in queues}
    total, clock, hist = {}, {}, {}

    def ap(name, a=None, b=None, P=None, third=None):
        shape = SCRATCH[name][1]
        p = slice(0, shape[0]) if P is None else slice(0, P)
        if len(shape) == 2:
            lo, hi, st = (0, shape[1], 1) if a is None else (a if isinstance(a, tuple) else (a, b, 1))
            return (T[name][p, slice(lo, hi) if st == 1 else slice(lo, hi, st)], [(name, lo, hi, st)])
        w = shape[2]
        k0, k1 = third if third else (0, w)
        if b is None:
            return (T[name][p, a, k0:k1], [(name, a * w + k0, a * w + k1, 1)])
        return (T[name][p, a:b, k0:k1], [(name, a * w + k0, (b - 1) * w + k1, 1)])

    def ind(win, off):
        return (win[0].indirect(off[0]), win[1] + off[1])

    def order(q, rw):
        want = {}
        for (name, lo, hi, st), isw in rw:
            ps = SCRATCH[name][0] == "psum"
            for (l2, h2, s2, w2, q2, sem, val) in hist.get(name, []):
                same = q2 == q
                if ps and not same:
                    if not (lo // 512 <= (h2 - 1) // 512 and l2 // 512 <= (hi - 1) // 512):
                        continue
                else:
                    if lo >= h2 or l2 >= hi or (st > 1 and st == s2 and (lo - l2) % st):
                        continue
                    if not (isw or w2) or (same and q == "t"):
                        continue
                if want.get(sem, 0) < val:
                    want[sem] = val
        k = know[q]
        for sem in sorted(want, key=lambda s: -len(clock[(s, want[s])])):
            if k.get(sem, 0) < want[sem]:
                queues[q].wait_ge(T.sem[sem], want[sem])
                for s2, v2 in clock[(sem, want[sem])].items():
                    if k.get(s2, 0) < v2:
                        k[s2] = v2

    def note(owner, sem, val, rw, c):
        total[sem] = val
        c[sem] = val
        clock[(sem, val)] = c
        for (name, lo, hi, st), isw in rw:
            keep = []
            for e in hist.get(name, []):
                inside = lo <= e[0] and e[1] <= hi and (st == 1 or (st == e[2] and (lo - e[0]) % st == 0))
                if not (inside and (isw or (not e[3] and e[4] == owner))):
                    keep.append(e)
            keep.append((lo, hi, st, isw, owner, sem, val))
            hist[name] = keep

    def both(reads, writes):
        return [(x, False) for r in reads for x in r[1]] + [(x, True) for r in writes for x in r[1]]

    def emit(q, reads, writes, call):
        rw = both(reads, writes)
        order(q, rw)
        sem = csem[q]
        call().then_inc(T.sem[sem], 1)
        note(q, sem, total.get(sem, 0) + 1, rw, dict(know[q]))

    def dma(q, sem, out, in_, reads, writes):
        rw = both(reads, writes)
        order(q, rw)
        queues[q].dma_start(out, in_).then_inc(T.sem[sem], 16)
        note("d" + sem, sem, 16, rw, dict(know[q]))

    def load(q, sem, buf, x):
        dma(q, sem, buf[0], x, [], [buf])

    def send(dst, dst_ap, src, rsem):
        order("g", both([src], []))
        rid, pid, _ = topo.addr(dst)
        g.remote_dma(dst_ap, src[0], T.sem[rsem], T.sem["ls"], pid, rid, topo.mask(core, dst))
        total["ls"] = total.get("ls", 0) + len(topo.engines(core, dst))

    def landing(name, sem, src):
        note("r" + sem, sem, len(topo.engines(src, core)), both([], [ap(name)]), {})

    def tt(out, a, b, op):
        emit("v", [a, b], [out], lambda: g.vector.tensor_tensor(out[0], a[0], b[0], op))

    def ts(out, a, s1, op0, s2=None, op1=None):
        rd = [a] + [s for s in (s1, s2) if isinstance(s, tuple)]
        x1, x2 = [s[0] if isinstance(s, tuple) else s for s in (s1, s2)]
        more = [] if op1 is None else [op1]
        emit("v", rd, [out], lambda: g.vector.tensor_scalar(out[0], a[0], x1, x2, op0, *more))

    def cp(out, a):
        emit("v", [a], [out], lambda: g.vector.tensor_copy(out[0], a[0]))

    def fill(out, c):
        emit("v", [], [out], lambda: g.vector.memset(out[0], c))

    def act(out, a, func, scale=1.0):
        sc = scale[0] if isinstance(scale, tuple) else scale
        emit("s", [a] + ([scale] if isinstance(scale, tuple) else []), [out], lambda: g.scalar.activation(out[0], a[0], func, scale=sc))

    def mm(out, l, r, start, stop):
        emit("t", [l, r], [out], lambda: g.tensor.matmul(out[0], l[0], r[0], start, stop))

    def iota(out, pattern, base, cm):
        emit("g", [], [out], lambda: g.iota(out[0], pattern, base, cm))

    def asel(out, a, pattern, op, base, cm):
        emit("g", [a], [out], lambda: g.affine_select(out[0], a[0], pattern, op, 0.0, base, cm))

    cols = {"fw": {}, "iw": {}}

    def work(buf, name, n, a, b):
        c = cols[buf]
        if name not in c:
            c[name] = (sum(w for _, w in c.values()), n)
        o, w = c[name]
        return ap(buf, o + a, o + (w if b is None else b))

    def fw(name, n=12, a=0, b=None):
        return work("fw", name, n, a, b)

    def iw(name, n=12, a=0, b=None):
        return work("iw", name, n, a, b)

    def blk(name, i):
        return ap(name, 128 * i, 128 * i + 128)

    load("y", "dj", ap("jcs"), T.jc[:])
    load("s", "ds", ap("sr8"), T.sr[:])
    load("s", "df", ap("fin0"), T.fx[:])
    load("y", "dp0", ap("pks", 0, 1024), T.pk[:, 0:1024])
    load("y", "dp1", ap("pks", 1024, 2048), T.pk[:, 1024:2048])
    load("y", "dr", ap("rtb"), T.rt[:])
    for t in range(1, VI):
        landing("pkg%d" % t, "pk%d" % t, T.cores[(rank - t) % N])
        landing("fin%d" % t, "fa%d" % t, T.cores[(rank - 1) % N])

    kp, kp4096, kp16, par, Zc, Zn = [ap("cols", c, c + 1) for c in range(6)]
    fill(ap("onesb"), 1.0)
    fill(ap("ones32"), 1.0)
    iota(ap("pidx", 0, 1), [[0, 1]], 0, 1)
    sel = ap("Sel")
    asel(sel, ap("onesb", P=8), [[1, 128]], A.is_ge, 0, -16)
    asel(sel, sel, [[-1, 128]], A.is_ge, 15, 16)
    iota(ap("CPi"), [[0, 6], [1, 2], [0, 16]], 0, 0)
    mm(ap("mis", 0, 128), sel, sel, True, True)
    ts(ap("pidx", 1, 2), ap("pidx", 0, 1), 15, A.bitwise_and)
    ts(ap("pidx", 2, 3), ap("pidx", 0, 1), 4, A.arith_shift_right, 1, A.bitwise_and)
    cp(kp, ap("pidx", 1, 2))
    ts(kp4096, ap("pidx", 1, 2), 4096.0, mul)
    ts(kp16, ap("pidx", 1, 2), 16.0, mul)
    cp(par, ap("pidx", 2, 3))
    ts(ap("W65", 0, 128), ap("mis", 0, 128), 65536.0, mul)
    w = 128
    while w < 2048:
        cp(ap("W65", w, 2 * w), ap("W65", 0, w))
        w *= 2
    for h in range(2):
        o = ap("W65", 1024 * h, 1024 * h + 1024)
        asel(o, o, [[-1, 8], [0, 8], [1, 16]], eq, -8 * h, 0)
        act(ap("W32", 1024 * h, 1024 * h + 1024), o, AF.Copy, 2.0 ** -16)
    asel(ap("I32"), ap("ones32"), [[-1, 128]], eq, 0, 1)
    cp(ap("BDb"), ap("mis", 0, 128))
    cp(ap("BD32"), ap("mis", 0, 128))

    for n, a, b in (("KU", 0, 16), ("KU", 208, 224), ("TB", 0, 16), ("TC", 192, 208)):
        fill(ap(n, a, b), 0.0)
    ts(ap("KU", 16, 208), ap("jcs"), kp4096, add)
    cp(ap("srb"), ap("sr8"))
    mm(ap("Wp", 0, 192), sel, ap("srb"), True, True)
    ts(ap("OH"), ap("Wp", 0, 192), kp, eq)
    tt(ap("Q0"), ap("OH"), ap("KU", 16, 208), mul)
    for i in range(16):
        mm(ap("mis", 128, 140), blk("W32", i), ap("Q0", (i, 192, 16)), i == 0, i == 15)

    def tr(out, a):
        emit("v", [a], [out], lambda: g.vector.transpose(out[0], a[0]))
    tr(ap("TA"), ap("KU", 16, 208))
    tr(ap("TB", 16, 208), ap("KU", 32, 224))
    tr(ap("TC", 0, 192), ap("KU", 0, 192))
    ts(ap("M1"), ap("CPi"), par, eq)
    ts(ap("Me"), ap("CPi"), par, A.is_gt)
    ts(ap("Mo"), ap("CPi"), par, A.is_lt)
    tt(ap("t1"), ap("TA"), ap("M1"), mul)
    tt(ap("t2"), ap("TB", 0, 192), ap("Me"), mul)
    tt(ap("t3"), ap("TC", 16, 208), ap("Mo"), mul)
    tt(ap("t1"), ap("t1"), ap("t2"), add)
    tt(ap("pkg0", 0, 192), ap("t1"), ap("t3"), add)
    cp(ap("pkg0", 192, 204), ap("mis", 128, 140))

    def prep(t):
        cp(iw("m0"), ap("pkg%d" % t, 192, 204))
        ts(iw("c1n"), iw("m0"), 4095, A.bitwise_and)
        ts(iw("p1n"), iw("m0"), 12, A.arith_shift_right)
        cp(ap("c16n"), iw("c1n"))
    prep(0)
    for h in (0, 1024):
        ts(ap("pf", h, h + 1024), ap("pks", h, h + 1024), 4095, A.bitwise_and)
        ts(ap("pf", 2048 + h, 3072 + h), ap("pks", h, h + 1024), 12, A.arith_shift_right)
    cp(ap("Ib"), ap("I32"))
    ts(ap("nI"), ap("I32"), -1.0, mul)
    fill(ap("rst"), 0.0)
    fill(ap("rst", (0, 192, 16)), 33554432.0)
    fill(ap("pf", 4096, 4480), 0)
    fill(Zc, 0.0)
    fill(ap("zt"), 0.0)

    def late():
        for t in range(1, VI):
            send(T.cores[(rank + t) % N], T["pkg%d" % t][:], ap("pkg0"), "pk%d" % t)
        iota(ap("J256"), [[256, 12]], 0, 0)
        iota(ap("D24"), [[16, 24]], 4096, 0)
        iota(ap("x12"), [[1, 12]], 0, 0)
        iota(ap("i16"), [[0, 12], [1, 16]], 0, 0)
        iota(ap("r96"), [[16, 6], [1, 16]], 0, 0)
        for s in range(3):
            ts(fw("POS%d" % s, 12, 0, NV), ap("J256", 0, NV), kp16, add, 3072.0 * s, add)
            ts(fw("POS%d" % s, 12, NV, 12), ap("J256", NV, 12), kp, add, 3072.0 * s, add)
        fill(fw("D36", 36, 0, 12), 0.0)
        ts(fw("D36", 36, 12, 36), ap("D24"), kp, add)
        fill(fw("G", 72), 0.0)
        cp(ap("exo"), ap("x12"))
        ts(ap("DIAG"), ap("i16"), kp, eq)
        ts(ap("pm"), ap("i16", 0, 16), kp, eq)
        for i in range(16):
            act(blk("Vi", i), ap("BDb"), AF.Copy, ap("pm", i, i + 1))
        rn, ra, rs = fw("rn", 6), fw("ra", 6), fw("rs", 6)
        ts(rn, ap("r96", (0, 96, 16)), kp, add)
        cp(rs, rn)
        for b in range(1, 6):
            ts(ra, rn, 12.0 * b, A.is_ge, -12.0, mul)
            tt(rs, rs, ra, add)
        ts(rs, rs, 11.0, A.min)
        cp(ap("rk"), rs)
        ts(ra, rn, 36.0, A.is_ge, 12.0, mul)
        tt(rs, rs, ra, add)
        cp(ap("rp"), rs)

    nb = 16 * NV
    cb = [(j, j + 2) for j in range(NV, 12, 2)]
    vb = [(j, j + 2) for j in range(0, NV, 2)]
    Y1, odd1, ev1 = iw("Y1", 24), iw("Y1", 24, 0, 12), iw("Y1", 24, 12, 24)
    Y2, odd2, ev2 = iw("Y2", 24), iw("Y2", 24, 0, 12), iw("Y2", 24, 12, 24)
    CC, c2, c3 = iw("CC", 24), iw("ci0"), iw("CC", 24, 0, 12)
    p1, c1, kk1, kk2 = iw("p1"), iw("c1"), iw("kk1"), ap("kk2")
    o1, o2, T21, V1, V2 = fw("o1"), fw("o2"), fw("T21"), fw("V1"), fw("V2")
    SA, SAa, SAb = fw("SA", 24), fw("SA", 24, 0, 12), fw("SA", 24, 12, 24)

    def C(a, b):
        return fw("C", 72, a, b)
    for t in range(VI):
        fname = "fin%d" % t
        K1 = "pkg%d" % t
        dA, dB = fw("D36", 36, 12, 24), fw("D36", 36, 24, 36)
        cp(p1, iw("p1n"))
        cp(c1, iw("c1n"))
        for s in range(3):
            base = 3072 * s
            cp(ap("N16"), ind(ap("pf"), ap("c16n" if s == 0 else "c16_%d" % (s - 1))))
            if s == 2:
                ts(kk2, iw("mi1"), 12, A.arith_shift_right, 15, A.bitwise_and)
                cp(ap("kb"), kk2)
            for k in range(16):
                o, f = ap("FX", (k, 16 * nb, 16)), ap(fname, 0, nb)
                if k < KS:
                    act(o, f, AF.Copy)
                else:
                    cp(o, f)
            for (j0, j1) in cb:
                act(ap("GC", 256 * (j0 - NV), 256 * (j1 - NV)), ind(ap("rtb"), ap("N16", 16 * j0, 16 * j1)), AF.Copy)

            def pc(j0, j1, k):
                return ap("psC", j0 - NV, j1 - NV, third=(16 * k, 16 * k + 16))
            for (j0, j1) in cb:
                mm(ap("psC", j0 - NV, j1 - NV), ap("Ib"), ap("zt"), True, False)
                for k in range(16):
                    mm(pc(j0, j1, k), ap("nI"), ap(fname, 16 * j0, 16 * j1), False, False)
            for (j0, j1) in cb:
                for k in range(16):
                    mm(pc(j0, j1, k), ap("Ib"), ap("GC", (256 * (j0 - NV) + k, 256 * (j1 - NV), 16)), False, k == 15)
            for (j0, j1) in vb:
                tt(ap("dall", base + 256 * j0, base + 256 * j1), ind(ap("rtb"), ap("N16", 16 * j0, 16 * j1)), ap("FX", 256 * j0, 256 * j1), sub)

            def absv(b):
                for j in range(*vb[b]):
                    act(ap("D3", j), ap("dall", base + 256 * j, base + 256 * j + 256), AF.Abs)

            def absc(b):
                for j in range(*cb[b]):
                    act(ap("dall", base + 256 * j, base + 256 * j + 256), ap("psC", j - NV), AF.Abs)

            def key(j0, j1):
                o = ap("key", 16 * j0, 16 * j1)
                mm(o, ap("I32"), ap(K1, 16 * j0, 16 * j1), True, False)
                for i in range(16):
                    if j0 < NV:
                        r = ap("D3", j0, j1, third=(16 * i, 16 * i + 16))
                    else:
                        r = ap("dall", (base + 256 * j0 + i, base + 256 * j1, 16))
                    mm(o, blk("W65", i), r, False, i == 15)
            if s == 2:
                for i in range(16):
                    mm(ap("Wp", (i, 192, 16)), blk("Vi", i), ap("kb"), True, True)
            absv(0)
            absc(0)
            absv(1)
            absc(1)
            absv(2)
            absv(3)
            key(0, 4)
            key(NV, 12)
            key(4, NV)

            if s == 0:
                if t == 0:
                    late()
                else:
                    tt(fw("x"), kk2, ap("kk3"), eq)
                    tt(fw("xa"), fw("x"), o2, mul)
                    tt(fw("xb"), o2, fw("xa"), sub)
                    tt(fw("xc"), fw("xb"), fw("T", 72, 0, 12), sub)
                    tt(ap("o3b"), fw("xc"), fw("T", 72, 36, 48), sub)
                    mm(ap("mis", 0, 12), ap("onesb"), ap("o3b"), True, True)
                    emit("v", [ap("mis", 0, 12)], [Zn], lambda: g.vector.tensor_reduce(Zn[0], ap("mis", 0, 12)[0], X, add))
                    tt(Zc, Zc, Zn, add)
                for i in range(16):
                    mm(ap("mis", 128, 140), blk("W65", i), ap(fname, (i, 192, 16)), i == 0, i == 15)
                ts(iw("d0z"), ap("mis", 128, 140), 2.0 ** -16, mul, Zc, add)
            if s == 1:
                ts(kk1, iw("mi0"), 12, A.arith_shift_right, 15, A.bitwise_and)
                ts(iw("d1"), iw("mi0"), 16, A.arith_shift_right)
                tt(fw("Ly"), fw("POS1"), fw("L0"), sub)
                tt(o1, kk1, p1, A.not_equal)
                tt(iw("x1"), iw("d1"), iw("d0z"), add)
                ts(fw("V1a"), kk1, 8192.0, mul)
                ts(iw("d1z"), iw("d1"), Zc, add)
                tt(fw("Lya"), fw("Ly"), o1, mul)
                ts(odd1, iw("x1"), 1, A.bitwise_and)
                tt(V1, fw("V1a"), c1, add)
                ts(fw("q"), o1, -16.0, mul, 16.0, add)
                tt(fw("Lb1"), fw("Lya"), fw("L0"), add)
                ts(ev1, odd1, -1.0, mul, 1.0, add)
                tt(fw("VA1"), V1, dA, sub)
                tt(fw("p1x"), fw("q"), p1, add)
                tt(fw("k1x"), fw("q"), kk1, add)
                ts(fw("G", 72, 0, 24), Y1, 8192.0, mul)
                tt(SAa, V1, ev1, mul)
                tt(SAb, fw("VA1"), odd1, mul)
                if t + 1 < VI:
                    prep(t + 1)
            if s == 2:
                ts(iw("d2"), iw("mi1"), 16, A.arith_shift_right)
                tt(T21, kk2, fw("p1x"), eq)
                tt(fw("e22"), kk2, fw("k1x"), eq)
                ts(fw("V2a"), kk2, 8192.0, mul)
                tt(iw("x2"), iw("d2"), iw("d1z"), add)
                tt(fw("o2a"), o1, T21, sub)
                tt(V2, fw("V2a"), c2, add)
                ts(odd2, iw("x2"), 1, A.bitwise_and)
                tt(o2, fw("o2a"), fw("e22"), sub)
                tt(fw("Lu"), fw("POS2"), fw("L1"), sub)
                ts(ap("EQ", 384, 576), ap("Wp", 0, 192), kp, eq, 8192.0, mul)
                ts(ev2, odd2, -1.0, mul, 1.0, add)
                ts(fw("qb"), o2, -16.0, mul, 16.0, add)
                tt(C(24, 36), V2, dB, sub)
                tt(fw("Lv"), fw("Lu"), o2, mul)
                tt(ap("P24", 0, 12), fw("qb"), p1, add)
                tt(ap("P24", 12, 24), fw("qb"), kk1, add)
                tt(ap("Bv", 384, 576), ind(ap("pf"), ap("c16_0")), ap("EQ", 384, 576), sub)
                cp(ap("P"), ind(ap("P24"), ap("rp", 0, 5)))
                tt(fw("Lb"), fw("Lv"), fw("L1"), add)
                tt(iw("CC", 24, 12, 24), c3, dA, sub)
                tt(fw("eV"), V2, ev2, mul)
                tt(fw("x3"), V2, odd1, mul)
                tt(fw("x4"), C(24, 36), ev1, mul)
                tt(fw("CA", 24), Y1, CC, mul)
                tt(fw("CB", 24), Y2, CC, mul)
                tt(C(60, 72), C(24, 36), odd2, mul)
                ts(fw("G", 72, 36, 60), Y2, 8192.0, mul)
                tt(fw("x5"), fw("x3"), SAa, add)
                tt(fw("X36", 36, 12, 24), SAb, T21, mul)
                tt(fw("X36", 36, 24, 36), fw("x4"), T21, mul)
                tt(C(0, 24), fw("CA", 24), SA, add)
                tt(C(36, 48), fw("CB", 24, 0, 12), fw("eV"), add)
                tt(fw("X36", 36, 0, 12), fw("x5"), T21, mul)
                cp(C(48, 60), fw("CB", 24, 12, 24))
                tt(fw("BX", 36), fw("X36", 36), fw("D36", 36), add)

            kr = ap("key", 0, 192)
            emit("v", [ap("rst"), kr], [ap("run")], lambda: g.vector.tensor_tensor_scan(ap("run")[0], ap("rst")[0], kr[0], 0.0, A.max, A.min))
            mn, kn = "mi%d" % s, "kL%d" % s
            mi, kL = iw(mn), iw(kn)
            cp(mi, ap("run", (15, 192, 16)))
            if s < 2:
                ts(c2 if s == 0 else c3, mi, 4095, A.bitwise_and)
            ts(iw(kn, 12, 0, NV), iw(mn, 12, 0, NV), 12, A.arith_shift_right, 15, A.bitwise_and)
            ts(iw(kn, 12, NV, 12), iw(mn, 12, NV, 12), 8, A.arith_shift_right, 240, A.bitwise_and)
            if s < 2:
                cp(ap("c16_%d" % s), c2 if s == 0 else c3)
                if s == 1:
                    tt(iw("kLo"), kL, o1, mul)
                    kL = iw("kLo")
                tt(fw("L%d" % s), kL, fw("POS0" if s == 0 else "Lb1"), add)
                cp(ap("L16"), fw("L%d" % s))
                fname = "fa" if s == 0 else "fb"
                act(ap(fname), ind(ap("dall", 0, base + 3072), ap("L16")), AF.Abs)
            else:
                tt(fw("Lz"), kL, o2, mul)
                ts(ap("kk3"), mi, 12, A.arith_shift_right, 15, A.bitwise_and)
                tt(fw("Lw"), fw("Lz"), fw("Lb"), add)
                cp(ap("K"), ind(ap("kk3"), ap("rk", 0, 5)))
                cp(ap("L16"), fw("Lw"))
                fo = ap("fo%d" % t)
                act(fo, ind(ap("dall"), ap("L16")), AF.Abs)
        if t + 1 < VI:
            send(T.cores[(rank + 1) % N], T["fin%d" % (t + 1)][:], fo, "fa%d" % (t + 1))
        else:
            dma("y", "dyf", T.yf[:], fo[0], [fo], [])

        tt(fw("T", 72), ap("K", 0, 72), ap("P", 0, 72), eq)
        tt(fw("H", 72), ap("K", 0, 72), fw("G", 72), mul)
        tt(fw("Ha", 72), fw("H", 72), fw("C", 72), add)
        tt(fw("Hb", 72), fw("Ha", 72), fw("T", 72), mul)
        tt(fw("Hc", 36), fw("Hb", 72, 0, 36), fw("Hb", 72, 36, 72), add)
        tt(iw("sel", 36), fw("Hc", 36), fw("BX", 36), add)
        ts(ap("sk"), iw("sel", 36), 13, A.arith_shift_right)
        ts(iw("sc", 36), iw("sel", 36), 8191, A.bitwise_and)
        tt(ap("R"), ind(ap("sk"), ap("exo")), ap("DIAG"), mul)
        mm(ap("U", 512, 704), ap("BDb"), ap("R"), True, True)
        cp(ap("cl16"), iw("sc", 36))
        cp(ap("kA"), ap("sk", 12, 24))
        for i in range(16):
            mm(ap("U", (i, 192, 16)), blk("Vi", i), ap("kA"), True, True)
        ts(ap("EQ", 0, 192), ap("U", 512, 704), kp, eq, 8192.0, mul)
        tt(ap("Bv", 0, 192), ind(ap("pf"), ap("cl16", 0, 12)), ap("EQ", 0, 192), sub)
        ts(ap("Qs"), ap("Bv", 0, 192), 0.0, A.min)
        mm(ap("Wp", 0, 192), ap("BD32"), ap("Qs"), True, False)
        mm(ap("Wp", 0, 192), ap("Ib"), ap("EQ", 384, 576), False, True)
        ts(ap("EQ", 192, 384), ap("U", 0, 192), kp, eq, 8192.0, mul)
        mm(ap("U", 192, 384), ap("BD32"), ap("Qs"), True, False)
        mm(ap("U", 192, 384), ap("Ib"), ap("EQ", 192, 384), False, True)
        tt(ap("Bv", 192, 384), ind(ap("pf"), ap("cl16", 12, 24)), ap("EQ", 192, 384), sub)
        tt(ap("newv", 192, 384), ap("Bv", 384, 576), ap("Wp", 0, 192), A.max)
        tt(ap("newv", 0, 192), ap("Bv", 192, 384), ap("U", 192, 384), A.max)
        pfo = ind(ap("pf"), ap("cl16", 12, 36))
        emit("v", [ap("newv"), ap("cl16", 12, 36)], [ap("pf")], lambda: g.vector.tensor_copy(pfo[0], ap("newv")[0]))

    for q in range(4):
        o, u = 512 * q, 512 * (q % 2)
        ts(ap("U", u, u + 512), ap("pf", 2048 + o, 2560 + o), 4096.0, mul)
        tt(ap("yps", o, o + 512), ap("pf", o, o + 512), ap("U", u, u + 512), add)
        dma("y", "dy%d" % q, T.yp[:, o:o + 512], ap("yps", o, o + 512)[0], [ap("yps", o, o + 512)], [])
    for sem in SEMAPHORES:
        if total.get(sem, 0) > know["g"].get(sem, 0):
            g.wait_ge(T.sem[sem], total[sem])
